import numpy as np
import ml_dtypes


def mxq(x, axis, fmt="e4m3"):
    dtype, down = {"e4m3": (ml_dtypes.float8_e4m3fn, 7), "e5m2": (ml_dtypes.float8_e5m2, 14)}[fmt]
    v = np.moveaxis(np.asarray(x, np.float32).astype(ml_dtypes.bfloat16).astype(np.float64), axis, -1)
    blocks = v.reshape(v.shape[:-1] + (-1, 32))
    amax = np.abs(blocks).max(-1, keepdims=True)
    byte = np.maximum(np.where(amax > 0, np.frexp(amax)[1] - 1 + 127, 0) - down, 1)
    scale = np.exp2(byte - 127.0)
    codes = (blocks / scale).astype(np.float32).astype(dtype).astype(np.float64)
    return np.moveaxis((codes * scale).reshape(v.shape), -1, axis)


WIDE = False


def mx_kscale(k):
    if not WIDE:
        return np.ones(k)
    levels = np.array([10, -10, 5, -5, 0])
    if k % 512:
        return np.exp2(np.random.permutation(np.resize(levels, k // 32))).repeat(32)
    a = np.empty((k // 512, 16))
    for p in range(k // 512):
        a[p, :8] = np.random.permutation(np.resize(levels, 8))
        for g in range(8):
            far = levels[np.abs(levels - a[p, g]) >= 10]
            a[p, g + 8] = far[np.random.randint(len(far))]
    return np.exp2(a.ravel()).repeat(32)


def f64(x):
    return np.asarray(x).astype(np.float64)


def striped(idx):
    return np.tile(idx.reshape(-1, 16).T, (8, 1)).astype(np.uint16)


def unstriped(offs):
    return offs[:16].T.reshape(-1).astype(np.int64)


E2M1 = np.array([0.0, 0.5, 1.0, 1.5, 2.0, 3.0, 4.0, 6.0, -0.0, -0.5, -1.0, -1.5, -2.0, -3.0, -4.0, -6.0])


def pack_weight(w, fmt):
    k, n = w.shape
    w = f64(np.asarray(w, np.float32).astype(ml_dtypes.bfloat16)).reshape(k // 32, 32, n)
    amax = np.abs(w).max(1)
    if fmt == "e4m3":
        byte = np.frexp(amax)[1] - 1 + 127 - 7
    else:
        mant, ex = np.frexp(amax / 6.0)
        byte = np.where(mant > 0.5, ex, ex - 1) + 127
    byte = np.clip(np.where(amax > 0, byte, 1), 1, 254)
    scaled = (w * np.exp2(127.0 - byte)[:, None, :]).reshape(k, n).astype(np.float32)
    by_word = np.ascontiguousarray(scaled.reshape(k // 512, 128, 4, n).transpose(0, 1, 3, 2))
    if fmt == "e4m3":
        words = by_word.astype(ml_dtypes.float8_e4m3fn).view(np.uint8)
    else:
        c = by_word.astype(ml_dtypes.float4_e2m1fn).view(np.uint8) & 0xF
        words = (c[..., 0::2] | (c[..., 1::2] << 4)).reshape(k // 512, 128, 2 * n)
    return np.ascontiguousarray(words), np.ascontiguousarray(byte.astype(np.uint8).reshape(k // 512, 16, n))


def unpack_weight(words, scales, fmt):
    g, _, n = scales.shape
    words = np.ascontiguousarray(words).reshape(g, 128, n, -1)
    if fmt == "e4m3":
        vals = words.view(ml_dtypes.float8_e4m3fn).astype(np.float64)
    else:
        nib = np.empty((g, 128, n, 4), np.uint8)
        nib[..., 0::2] = words & 0xF
        nib[..., 1::2] = words >> 4
        vals = E2M1[nib]
    vals = vals * np.repeat(np.exp2(scales.astype(np.float64) - 127.0), 8, axis=1)[..., None]
    return vals.transpose(0, 1, 3, 2).reshape(g * 512, n)


def gelu(v):
    return 0.5 * v * (1.0 + np.tanh(np.sqrt(2.0 / np.pi) * (v + 0.044715 * v**3)))


K, H, T, S, T2, P = 1024, 1024, 2048, 512, 1024, 512

def setup_inputs():
    n = np.random.standard_normal
    s = mx_kscale(K)[:, None]
    u = mx_kscale(H)[:, None]
    d = {}
    d["tab_words"], d["tab_scales"] = pack_weight(n((K, T)) * s, "e4m3")
    d["offs"] = striped(np.random.permutation(T)[:S])
    d["wa"] = (n((K, H)) / K ** 0.5 / s * u.T).astype(np.float32)
    d["wb_words"], d["wb_scales"] = pack_weight(1.6 * n((K, H)) / K ** 0.5 / s, "e4m3")
    d["gain"] = (1.2 * np.exp(0.3 * n(H)) * u[:, 0]).astype(np.float32)
    d["page0"] = (n((H, T2)) * u).astype(np.float32)
    d["wgs"] = np.exp(0.3 * n((128, S))).astype(np.float32)
    d["offs2"] = striped(np.random.permutation(T2)[:S])
    d["offs3"] = striped(np.random.permutation(T2)[:P])
    d["curl"] = np.exp(0.4 * n(H)).astype(np.float32)
    d["wc"] = (n((H, H)) / H ** 0.5 / u).astype(np.float32)
    d["wd_words"], d["wd_scales"] = pack_weight(n((H, H)) / H ** 0.5 / u, "e2m1")
    d["offs4"] = striped(np.random.permutation(T2)[:P])
    d["quire"] = (np.exp(0.3 * n(H)) / u[:, 0]).astype(np.float32)
    return d

def reference(tab_words, tab_scales, offs, wa, wb_words, wb_scales, gain, page0, wgs,
              offs2, offs3, curl, wc, wd_words, wd_scales, offs4, quire):
    v = unpack_weight(tab_words, tab_scales, "e4m3")[:, unstriped(offs)]
    a = mxq(f64(wa), 0, "e4m3").T @ v
    b = unpack_weight(wb_words, wb_scales, "e4m3").T @ v
    h = f64(gain)[:, None] * (b / (1.0 + np.exp(-b))) - np.abs(a)
    page = f64(page0).copy()
    page[:, unstriped(offs2)] = np.tile(f64(wgs), (H // 128, 1)) * h
    x = mxq(page[:, unstriped(offs3)] * f64(curl)[:, None], 0, "e4m3")
    y1 = mxq(f64(wc), 0, "e4m3").T @ x
    y2 = unpack_weight(wd_words, wd_scales, "e2m1").T @ x
    same = page[:, unstriped(offs4)] * f64(quire)[:, None]
    return np.maximum(y1, same) - np.abs(y2)

@@ -1,0 +1,301 @@
+from contextlib import ExitStack
+
+import concourse.mybir as mybir
+from concourse.masks import make_identity
+
+K, H, T, S, T2, NP = 1024, 1024, 2048, 512, 1024, 512
+FLOPS = 4 * 2 * K * H * S
+
+F32 = mybir.dt.float32
+BF16 = mybir.dt.bfloat16
+I32 = mybir.dt.int32
+U32 = mybir.dt.uint32
+U16 = mybir.dt.uint16
+U8 = mybir.dt.uint8
+FP8X4 = mybir.dt.float8_e4m3fn_x4
+FP4X4 = mybir.dt.float4_e2m1fn_x4
+ALU = mybir.AluOpType
+ACT = mybir.ActivationFunctionType
+
+P = 128
+PACK = 4
+KP = P * PACK
+PASSES = K // KP
+TILES = H // P
+QUADS = 4
+WA_CHUNKS = [(0, 128), (128, 128), (256, 256), (512, 256), (768, 256)]
+WC_CHUNK = 256
+GPSIMD_SUBS = 0
+WC_RAW_TAGS = ["wa_raw2_%d", "wa_raw3_%d", "wc_raw2_%d", "wa_raw4_%d"]
+
+
+def tile_list_folio_condition_page_kernel(
+    tc, tab_words, tab_scales, offs, wa, wb_words, wb_scales, gain, page0, wgs,
+    offs2, offs3, curl, wc, wd_words, wd_scales, offs4, quire, out,
+):
+    nc = tc.nc
+    with ExitStack() as ctx:
+        keep = ctx.enter_context(tc.tile_pool(name="keep", bufs=1))
+        ring = ctx.enter_context(tc.tile_pool(name="ring", bufs=2))
+        psum = ctx.enter_context(tc.psum_pool(name="psum", bufs=8))
+
+        def held(shape, dtype, name, tag=None):
+            return keep.tile(shape, dtype, name=name, tag=tag or name, align_bytes=64)
+
+        def load_list(src, name):
+            lst = held([P, S // 16], U16, name)
+            nc.sync.dma_start(lst[:], src)
+            return lst
+
+        def load_raw(w, a, c0, width, name, tag=None):
+            raw = held([P, PACK, width], F32, name, tag)
+            rows = w[a * KP : (a + 1) * KP, c0 : c0 + width]
+            nc.sync.dma_start(out=raw[:], in_=rows.rearrange("(p j) c -> p j c", j=PACK))
+            return raw
+
+        def load_tab_words(a):
+            words = held([P, T], U32, "tab_w%d" % a)
+            nc.sync.dma_start(out=words[:].bitcast(I32), in_=tab_words[a].rearrange("p t i -> p (t i)").bitcast(I32))
+            return words
+
+        def load_wb_words(c):
+            c0, width = WA_CHUNKS[c]
+            words = held([P, PASSES, width], U32, "wb_w%d" % c)
+            src = wb_words[:, :, c0 : c0 + width, :].rearrange("a p c i -> p a (c i)")
+            nc.sync.dma_start(out=words[:].bitcast(I32), in_=src.bitcast(I32))
+            return words
+
+        def load_page(t):
+            page = held([P, T2], F32, "page%d" % t)
+            nc.sync.dma_start(out=page[:], in_=page0[t * P : (t + 1) * P, :])
+            return page
+
+        def load_packed_scales(engine, plane, scales):
+            for q in range(QUADS):
+                engine.dma_start(
+                    out=plane[32 * q : 32 * q + 4 * PASSES, :].bitcast(I32),
+                    in_=scales[:, 4 * q : 4 * q + 4, :].bitcast(I32),
+                )
+
+        tab_s = held([P, T], U8, "tab_s")
+        nc.vector.memset(tab_s[:].bitcast(I32), 0)
+        ident = held([P, P], F32, "ident")
+        make_identity(nc, ident[:])
+        vec_rows = held([P, P], F32, "vec_rows")
+        nc.gpsimd.memset(vec_rows[:], 0.0)
+        for n, vec in enumerate((gain, curl, quire)):
+            nc.gpsimd.dma_start(out=vec_rows[TILES * n : TILES * (n + 1), :], in_=vec.rearrange("(t p) -> t p", p=P))
+        wb_s = held([P, H], U8, "wb_s")
+        nc.vector.memset(wb_s[:].bitcast(I32), 0)
+        wd_s = held([P, PASSES, H], U8, "wd_s")
+        nc.vector.memset(wd_s[:].rearrange("p a c -> p (a c)").bitcast(I32), 0)
+
+        list1 = load_list(offs, "list1")
+        tab_w = [load_tab_words(0)]
+        load_packed_scales(nc.sync, tab_s, tab_scales)
+        wa_raw = [[load_raw(wa, a, 0, WA_CHUNKS[0][1], "wa_raw0_%d" % a) for a in range(PASSES)]]
+        tab_w.append(load_tab_words(1))
+        wb_w = [load_wb_words(0)]
+        load_packed_scales(nc.sync, wb_s, wb_scales)
+        list2 = load_list(offs2, "list2")
+        wgs_sb = held([P, S], F32, "wgs_sb")
+        nc.sync.dma_start(out=wgs_sb[:], in_=wgs)
+        pages = [load_page(0)]
+        list3 = load_list(offs3, "list3")
+        wc_raw = []
+
+        def load_wa(c):
+            c0, width = WA_CHUNKS[c]
+            wa_raw.append([load_raw(wa, a, c0, width, "wa_raw%d_%d" % (c, a)) for a in range(PASSES)])
+            wb_w.append(load_wb_words(c))
+
+        load_wa(1)
+        load_wa(2)
+        pages.append(load_page(1))
+        pages.append(load_page(2))
+        load_wa(3)
+        pages.append(load_page(3))
+        load_wa(4)
+        for t in range(4, TILES):
+            pages.append(load_page(t))
+        list4 = load_list(offs4, "list4")
+
+        def interleave(dst, src):
+            nc.scalar.copy(
+                out=dst.rearrange("p (c i) j -> p c j i", i=4),
+                in_=src.rearrange("p j (c i) -> p c j i", i=4),
+            )
+
+        def round_weight(raws, width, name):
+            grouped = held([P, PASSES, width, PACK], BF16, name + "_grouped")
+            for a in range(PASSES):
+                interleave(grouped[:, a], raws[a][:])
+            return grouped[:].rearrange("p a c j -> p (a c j)")
+
+        def quantise(flat, width, name):
+            codes = held([P, width], U32, name + "_codes")
+            plane = held([P, width], U8, name + "_plane")
+            nc.vector.quantize_mx(out=codes[:].bitcast(FP8X4), scales=plane[:], in_=flat)
+            return codes, plane
+
+        vec_ps = psum.tile([P, S], F32, name="acc")
+        nc.tensor.transpose(vec_ps[:, 0:P], vec_rows[:], ident[:])
+        vecs = held([P, 3 * TILES], F32, "vecs")
+
+        v_w = [held([P, S], U32, "v_w%d" % a) for a in range(PASSES)]
+        v_s = held([P, S], U8, "v_s")
+        nc.vector.tensor_copy(v_w[0][:], tab_w[0][:].indirect(list1[:]))
+        wa_q = {}
+        wc_q = {}
+
+        def prep_wa(c):
+            width = WA_CHUNKS[c][1]
+            wa_q[c] = quantise(round_weight(wa_raw[c], width, "wa%d" % c), PASSES * width, "wa%d" % c)
+
+        def prep_wc(c):
+            wc_q[c] = quantise(round_weight(wc_raw[c], WC_CHUNK, "wc%d" % c), PASSES * WC_CHUNK, "wc%d" % c)
+
+        def load_wc(c):
+            tags = [WC_RAW_TAGS[c] % a for a in range(PASSES)]
+            wc_raw.append([load_raw(wc, a, c * WC_CHUNK, WC_CHUNK, "wc_raw%d_%d" % (c, a), tags[a]) for a in range(PASSES)])
+
+        prep_wa(0)
+        nc.vector.tensor_copy(v_s[:], tab_s[:].indirect(list1[:]))
+        nc.vector.tensor_copy(v_w[1][:], tab_w[1][:].indirect(list1[:]))
+        nc.scalar.copy(out=vecs[:], in_=vec_ps[:, 0 : 3 * TILES])
+
+        def chunk_of(t):
+            for c, (c0, width) in enumerate(WA_CHUNKS):
+                if c0 <= t * P < c0 + width:
+                    return c, t * P - c0, width
+
+        first = {}
+        abs_a = held([P, TILES, S], F32, "abs_a", tag="abs_then_same")
+
+        def stage1(t):
+            c, off, width = chunk_of(t)
+            acc_b = psum.tile([P, S], F32, name="acc")
+            acc_a = psum.tile([P, S], F32, name="acc")
+            codes, plane = wa_q[c]
+            for a in range(PASSES):
+                nc.tensor.matmul_mx(
+                    out=acc_b[:], lhsT=wb_w[c][:, a, off : off + P].bitcast(FP8X4),
+                    lhsT_scale=wb_s[4 * a : P, t * P : (t + 1) * P],
+                    rhs=v_w[a][:].bitcast(FP8X4), rhs_scale=v_s[4 * a : P, :],
+                    start=(a == 0), stop=(a == PASSES - 1),
+                )
+            for a in range(PASSES):
+                cols = slice(a * width + off, a * width + off + P)
+                nc.tensor.matmul_mx(
+                    out=acc_a[:], lhsT=codes[:, cols].bitcast(FP8X4), lhsT_scale=plane[:, cols],
+                    rhs=v_w[a][:].bitcast(FP8X4), rhs_scale=v_s[4 * a : P, :],
+                    start=(a == 0), stop=(a == PASSES - 1),
+                )
+            silu_b = held([P, S], F32, "silu%d" % t)
+            nc.scalar.activation(out=silu_b[:], in_=acc_b[:], func=ACT.Silu)
+            nc.scalar.activation(out=abs_a[:, t, :], in_=acc_a[:], func=ACT.Abs)
+            first[t] = silu_b
+
+        picked = {}
+
+        def change_page(t):
+            if t in (1, 3, 5):
+                h = held([P, S], F32, "h%d" % t, tag="wa%d_grouped" % (2 + t // 2))
+            else:
+                h = ring.tile([P, S], F32, name="h")
+            nc.vector.scalar_tensor_tensor(
+                out=h[:], in0=first[t][:], scalar=vecs[:, t : t + 1], in1=abs_a[:, t, :], op0=ALU.mult, op1=ALU.subtract
+            )
+            nc.vector.tensor_tensor(pages[t][:].indirect(list2[:]), h[:], wgs_sb[:], ALU.mult)
+            picked[t] = held([P, NP], F32, "picked%d" % t)
+            nc.vector.tensor_copy(picked[t][:], pages[t][:].indirect(list3[:]))
+
+        x_rows = {}
+        x_nat = {}
+
+        def scale_x(t):
+            b, u = divmod(t, QUADS)
+            if u == 0:
+                x_nat[b] = held([P, QUADS, NP], BF16, "x_nat%d" % b, tag="wa_raw4_%d" % (1 - b))
+            nc.scalar.activation(out=x_nat[b][:, u, :], in_=picked[t][:], func=ACT.Copy, scale=vecs[:, TILES + t : TILES + t + 1])
+            if u == 0:
+                x_rows[b] = held([P, PACK, NP], BF16, "x_rows%d" % b, tag="wa_raw%d_0" % (2 + b))
+            nc.sync.dma_start(out=x_rows[b][32 * u : 32 * (u + 1)].rearrange("p j n -> p (j n)"), in_=x_nat[b][:, u, :])
+
+        x_q = {}
+
+        def quantise_x(b):
+            grouped = held([P, NP, PACK], BF16, "x_grouped%d" % b, tag="wa_raw%d_1" % (2 + b))
+            interleave(grouped[:], x_rows[b][:])
+            x_q[b] = quantise(grouped[:].rearrange("p n j -> p (n j)"), NP, "x%d" % b)
+
+        stage1(0)
+        prep_wa(1)
+        stage1(1)
+        for t in range(TILES):
+            if t % 2 == 1 and t < 6:
+                prep_wa(2 + t // 2)
+            change_page(t)
+            if t >= 1 and t + 1 < TILES:
+                stage1(t + 1)
+        for c in range(H // WC_CHUNK):
+            load_wc(c)
+        wd_w = held([P, PASSES, 2 * H], U8, "wd_w")
+        nc.sync.dma_start(out=wd_w[:].bitcast(I32), in_=wd_words.rearrange("a p c -> p a c").bitcast(I32))
+        for q in range(QUADS):
+            nc.sync.dma_start(
+                out=wd_s[32 * q : 32 * q + 4, :, :].bitcast(I32),
+                in_=wd_scales[:, 4 * q : 4 * q + 4, :].rearrange("a r c -> r a c").bitcast(I32),
+            )
+        for c in range(H // WC_CHUNK):
+            prep_wc(c)
+        for t in range(TILES):
+            scale_x(t)
+        quantise_x(0)
+
+        same_a = held([P, TILES - 2, NP], F32, "same_a", tag="abs_then_same")
+        second = {}
+
+        def stage2(t, b):
+            if b == 0:
+                second[t] = (psum.tile([P, NP], F32, name="acc"), psum.tile([P, NP], F32, name="acc"))
+            y1, y2 = second[t]
+            c, off = divmod(t * P, WC_CHUNK)
+            codes, plane = wc_q[c]
+            x_codes, x_plane = x_q[b]
+            cols = slice(b * WC_CHUNK + off, b * WC_CHUNK + off + P)
+            nc.tensor.matmul_mx(
+                out=y2[:], lhsT=wd_w[:, b, 2 * t * P : 2 * (t + 1) * P].bitcast(FP4X4),
+                lhsT_scale=wd_s[:, b, t * P : (t + 1) * P],
+                rhs=x_codes[:].bitcast(FP8X4), rhs_scale=x_plane[:],
+                start=(b == 0), stop=(b == PASSES - 1),
+            )
+            nc.tensor.matmul_mx(
+                out=y1[:], lhsT=codes[:, cols].bitcast(FP8X4), lhsT_scale=plane[:, cols],
+                rhs=x_codes[:].bitcast(FP8X4), rhs_scale=x_plane[:],
+                start=(b == 0), stop=(b == PASSES - 1),
+            )
+
+        def finish(t):
+            y1, y2 = second[t]
+            abs_y2 = held([P, NP], F32, "abs_y2_%d" % t, tag="silu%d" % t)
+            nc.scalar.activation(out=abs_y2[:], in_=y2[:], func=ACT.Abs)
+            top = held([P, NP], F32, "top%d" % t, tag="picked%d" % t)
+            nc.vector.scalar_tensor_tensor(
+                out=top[:], in0=same[t], scalar=vecs[:, 2 * TILES + t : 2 * TILES + t + 1], in1=y1[:],
+                op0=ALU.mult, op1=ALU.max,
+            )
+            res = held([P, NP], F32, "res%d" % t, tag="wc%d_grouped" % (t % 4))
+            engine = nc.gpsimd if t < GPSIMD_SUBS else nc.vector
+            engine.tensor_tensor(res[:], top[:], abs_y2[:], ALU.subtract)
+            nc.sync.dma_start(out=out[t * P : (t + 1) * P, :], in_=res[:])
+
+        quantise_x(1)
+        same_b = held([P, 2, NP], F32, "same_b", tag="wa_raw3_1")
+        same = [same_a[:, t, :] for t in range(TILES - 2)] + [same_b[:, t, :] for t in range(2)]
+        for t in range(TILES):
+            nc.vector.tensor_copy(same[t], pages[t][:].indirect(list4[:]))
+        for t in range(TILES):
+            stage2(t, 0)
+            stage2(t, 1)
+            finish(t)

@@ -25,7 +25,7 @@ TILES = H // P
 QUADS = 4
 WA_CHUNKS = [(0, 128), (128, 128), (256, 256), (512, 256), (768, 256)]
 WC_CHUNK = 256
-GPSIMD_SUBS = 0
+GPSIMD_SUBS = 7
 WC_RAW_TAGS = ["wa_raw2_%d", "wa_raw3_%d", "wc_raw2_%d", "wa_raw4_%d"]
 
 
@@ -93,10 +93,10 @@ def tile_list_folio_condition_page_kernel(
         list1 = load_list(offs, "list1")
         tab_w = [load_tab_words(0)]
         load_packed_scales(nc.sync, tab_s, tab_scales)
-        wa_raw = [[load_raw(wa, a, 0, WA_CHUNKS[0][1], "wa_raw0_%d" % a) for a in range(PASSES)]]
         tab_w.append(load_tab_words(1))
         wb_w = [load_wb_words(0)]
         load_packed_scales(nc.sync, wb_s, wb_scales)
+        wa_raw = [[load_raw(wa, a, 0, WA_CHUNKS[0][1], "wa_raw0_%d" % a) for a in range(PASSES)]]
         list2 = load_list(offs2, "list2")
         wgs_sb = held([P, S], F32, "wgs_sb")
         nc.sync.dma_start(out=wgs_sb[:], in_=wgs)
@@ -112,11 +112,9 @@ def tile_list_folio_condition_page_kernel(
         load_wa(1)
         load_wa(2)
         pages.append(load_page(1))
-        pages.append(load_page(2))
         load_wa(3)
-        pages.append(load_page(3))
         load_wa(4)
-        for t in range(4, TILES):
+        for t in range(2, TILES):
             pages.append(load_page(t))
         list4 = load_list(offs4, "list4")
 
@@ -150,7 +148,13 @@ def tile_list_folio_condition_page_kernel(
 
         def prep_wa(c):
             width = WA_CHUNKS[c][1]
-            wa_q[c] = quantise(round_weight(wa_raw[c], width, "wa%d" % c), PASSES * width, "wa%d" % c)
+            flat = round_weight(wa_raw[c], width, "wa%d" % c)
+            if c == 0:
+                parts = [quantise(flat[:, a * width * PACK : (a + 1) * width * PACK], width, "wa0_%d" % a) for a in range(PASSES)]
+                wa_q[c] = [(codes[:], plane[:]) for codes, plane in parts]
+            else:
+                codes, plane = quantise(flat, PASSES * width, "wa%d" % c)
+                wa_q[c] = [(codes[:, a * width : (a + 1) * width], plane[:, a * width : (a + 1) * width]) for a in range(PASSES)]
 
         def prep_wc(c):
             wc_q[c] = quantise(round_weight(wc_raw[c], WC_CHUNK, "wc%d" % c), PASSES * WC_CHUNK, "wc%d" % c)
@@ -159,9 +163,9 @@ def tile_list_folio_condition_page_kernel(
             tags = [WC_RAW_TAGS[c] % a for a in range(PASSES)]
             wc_raw.append([load_raw(wc, a, c * WC_CHUNK, WC_CHUNK, "wc_raw%d_%d" % (c, a), tags[a]) for a in range(PASSES)])
 
-        prep_wa(0)
         nc.vector.tensor_copy(v_s[:], tab_s[:].indirect(list1[:]))
         nc.vector.tensor_copy(v_w[1][:], tab_w[1][:].indirect(list1[:]))
+        prep_wa(0)
         nc.scalar.copy(out=vecs[:], in_=vec_ps[:, 0 : 3 * TILES])
 
         def chunk_of(t):
@@ -176,7 +180,6 @@ def tile_list_folio_condition_page_kernel(
             c, off, width = chunk_of(t)
             acc_b = psum.tile([P, S], F32, name="acc")
             acc_a = psum.tile([P, S], F32, name="acc")
-            codes, plane = wa_q[c]
             for a in range(PASSES):
                 nc.tensor.matmul_mx(
                     out=acc_b[:], lhsT=wb_w[c][:, a, off : off + P].bitcast(FP8X4),
@@ -185,9 +188,9 @@ def tile_list_folio_condition_page_kernel(
                     start=(a == 0), stop=(a == PASSES - 1),
                 )
             for a in range(PASSES):
-                cols = slice(a * width + off, a * width + off + P)
+                codes, plane = wa_q[c][a]
                 nc.tensor.matmul_mx(
-                    out=acc_a[:], lhsT=codes[:, cols].bitcast(FP8X4), lhsT_scale=plane[:, cols],
+                    out=acc_a[:], lhsT=codes[:, off : off + P].bitcast(FP8X4), lhsT_scale=plane[:, off : off + P],
                     rhs=v_w[a][:].bitcast(FP8X4), rhs_scale=v_s[4 * a : P, :],
                     start=(a == 0), stop=(a == PASSES - 1),
                 )
@@ -199,15 +202,19 @@ def tile_list_folio_condition_page_kernel(
         picked = {}
 
         def change_page(t):
-            if t in (1, 3, 5):
-                h = held([P, S], F32, "h%d" % t, tag="wa%d_grouped" % (2 + t // 2))
+            if t in (1, 2, 3):
+                h = held([P, S], F32, "h%d" % t, tag="wa%d_grouped" % (t + 1))
             else:
                 h = ring.tile([P, S], F32, name="h")
             nc.vector.scalar_tensor_tensor(
                 out=h[:], in0=first[t][:], scalar=vecs[:, t : t + 1], in1=abs_a[:, t, :], op0=ALU.mult, op1=ALU.subtract
             )
+            if t >= 1:
+                pick(t - 1)
             nc.vector.tensor_tensor(pages[t][:].indirect(list2[:]), h[:], wgs_sb[:], ALU.mult)
-            picked[t] = held([P, NP], F32, "picked%d" % t)
+
+        def pick(t):
+            picked[t] = held([P, NP], F32, "picked%d" % t, tag="silu%d" % (t + 1))
             nc.vector.tensor_copy(picked[t][:], pages[t][:].indirect(list3[:]))
 
         x_rows = {}
@@ -233,11 +240,12 @@ def tile_list_folio_condition_page_kernel(
         prep_wa(1)
         stage1(1)
         for t in range(TILES):
-            if t % 2 == 1 and t < 6:
-                prep_wa(2 + t // 2)
+            if t in (1, 2, 3):
+                prep_wa(t + 1)
             change_page(t)
             if t >= 1 and t + 1 < TILES:
                 stage1(t + 1)
+        pick(TILES - 1)
         for c in range(H // WC_CHUNK):
             load_wc(c)
         wd_w = held([P, PASSES, 2 * H], U8, "wd_w")
@@ -253,7 +261,18 @@ def tile_list_folio_condition_page_kernel(
             scale_x(t)
         quantise_x(0)
 
-        same_a = held([P, TILES - 2, NP], F32, "same_a", tag="abs_then_same")
+        same = {}
+
+        def pick_same(t, tile):
+            same[t] = tile
+            nc.vector.tensor_copy(tile, pages[t][:].indirect(list4[:]))
+
+        same_a = held([P, 2, NP], F32, "same_a", tag="abs_then_same")
+        same_b = held([P, 2, NP], F32, "same_b", tag="wa_raw2_1")
+        for t in range(2):
+            pick_same(t, same_a[:, t, :])
+        for t in range(2):
+            pick_same(2 + t, same_b[:, t, :])
         second = {}
 
         def stage2(t, b):
@@ -280,7 +299,7 @@ def tile_list_folio_condition_page_kernel(
             y1, y2 = second[t]
             abs_y2 = held([P, NP], F32, "abs_y2_%d" % t, tag="silu%d" % t)
             nc.scalar.activation(out=abs_y2[:], in_=y2[:], func=ACT.Abs)
-            top = held([P, NP], F32, "top%d" % t, tag="picked%d" % t)
+            top = ring.tile([P, NP], F32, name="top", bufs=4)
             nc.vector.scalar_tensor_tensor(
                 out=top[:], in0=same[t], scalar=vecs[:, 2 * TILES + t : 2 * TILES + t + 1], in1=y1[:],
                 op0=ALU.mult, op1=ALU.max,
@@ -290,12 +309,17 @@ def tile_list_folio_condition_page_kernel(
             engine.tensor_tensor(res[:], top[:], abs_y2[:], ALU.subtract)
             nc.sync.dma_start(out=out[t * P : (t + 1) * P, :], in_=res[:])
 
-        quantise_x(1)
-        same_b = held([P, 2, NP], F32, "same_b", tag="wa_raw3_1")
-        same = [same_a[:, t, :] for t in range(TILES - 2)] + [same_b[:, t, :] for t in range(2)]
-        for t in range(TILES):
-            nc.vector.tensor_copy(same[t], pages[t][:].indirect(list4[:]))
-        for t in range(TILES):
+        early = TILES // 2
+        for t in range(early):
             stage2(t, 0)
+        quantise_x(1)
+        pick_same(4, held([P, NP], F32, "same_c", tag="wa_raw3_1")[:])
+        for t in range(early):
             stage2(t, 1)
+        for t in range(TILES):
+            if t >= early:
+                stage2(t, 0)
+                stage2(t, 1)
             finish(t)
+            if t + 5 < TILES:
+                pick_same(t + 5, same[t])

@@ -25,7 +25,9 @@ TILES = H // P
 QUADS = 4
 WA_CHUNKS = [(0, 128), (128, 128), (256, 256), (512, 256), (768, 256)]
 WC_CHUNK = 256
-GPSIMD_SUBS = 7
+GPSIMD_SUBS = 6
+HALF = NP // 2
+FREE_PICKS = 3
 WC_RAW_TAGS = ["wa_raw2_%d", "wa_raw3_%d", "wc_raw2_%d", "wa_raw4_%d"]
 
 
@@ -37,6 +39,7 @@ def tile_list_folio_condition_page_kernel(
     with ExitStack() as ctx:
         keep = ctx.enter_context(tc.tile_pool(name="keep", bufs=1))
         ring = ctx.enter_context(tc.tile_pool(name="ring", bufs=2))
+        late = ctx.enter_context(tc.tile_pool(name="late", bufs=1))
         psum = ctx.enter_context(tc.psum_pool(name="psum", bufs=8))
 
         def held(shape, dtype, name, tag=None):
@@ -79,12 +82,17 @@ def tile_list_folio_condition_page_kernel(
 
         tab_s = held([P, T], U8, "tab_s")
         nc.vector.memset(tab_s[:].bitcast(I32), 0)
+        def load_vectors(vectors, name):
+            rows = held([P, P], F32, name)
+            nc.gpsimd.memset(rows[:], 0.0)
+            for n, vec in enumerate(vectors):
+                nc.gpsimd.dma_start(out=rows[TILES * n : TILES * (n + 1), :], in_=vec.rearrange("(t p) -> t p", p=P))
+            return rows
+
+        gain_rows = load_vectors([gain], "gain_rows")
         ident = held([P, P], F32, "ident")
         make_identity(nc, ident[:])
-        vec_rows = held([P, P], F32, "vec_rows")
-        nc.gpsimd.memset(vec_rows[:], 0.0)
-        for n, vec in enumerate((gain, curl, quire)):
-            nc.gpsimd.dma_start(out=vec_rows[TILES * n : TILES * (n + 1), :], in_=vec.rearrange("(t p) -> t p", p=P))
+        later_rows = load_vectors([curl, quire], "later_rows")
         wb_s = held([P, H], U8, "wb_s")
         nc.vector.memset(wb_s[:].bitcast(I32), 0)
         wd_s = held([P, PASSES, H], U8, "wd_s")
@@ -93,16 +101,11 @@ def tile_list_folio_condition_page_kernel(
         list1 = load_list(offs, "list1")
         tab_w = [load_tab_words(0)]
         load_packed_scales(nc.sync, tab_s, tab_scales)
-        tab_w.append(load_tab_words(1))
+        wa_raw = [[load_raw(wa, 0, 0, WA_CHUNKS[0][1], "wa_raw0_0")]]
         wb_w = [load_wb_words(0)]
+        tab_w.append(load_tab_words(1))
         load_packed_scales(nc.sync, wb_s, wb_scales)
-        wa_raw = [[load_raw(wa, a, 0, WA_CHUNKS[0][1], "wa_raw0_%d" % a) for a in range(PASSES)]]
-        list2 = load_list(offs2, "list2")
-        wgs_sb = held([P, S], F32, "wgs_sb")
-        nc.sync.dma_start(out=wgs_sb[:], in_=wgs)
-        pages = [load_page(0)]
-        list3 = load_list(offs3, "list3")
-        wc_raw = []
+        wa_raw[0].append(load_raw(wa, 1, 0, WA_CHUNKS[0][1], "wa_raw0_1"))
 
         def load_wa(c):
             c0, width = WA_CHUNKS[c]
@@ -110,24 +113,31 @@ def tile_list_folio_condition_page_kernel(
             wb_w.append(load_wb_words(c))
 
         load_wa(1)
+        list2 = load_list(offs2, "list2")
+        wgs_sb = held([P, S], F32, "wgs_sb")
+        nc.sync.dma_start(out=wgs_sb[:], in_=wgs)
+        pages = [load_page(0)]
+        list3 = load_list(offs3, "list3")
+        wc_raw = []
         load_wa(2)
         pages.append(load_page(1))
         load_wa(3)
+        pages.append(load_page(2))
         load_wa(4)
-        for t in range(2, TILES):
+        for t in range(3, TILES):
             pages.append(load_page(t))
         list4 = load_list(offs4, "list4")
 
-        def interleave(dst, src):
-            nc.scalar.copy(
+        def interleave(dst, src, copy=nc.scalar.copy):
+            copy(
                 out=dst.rearrange("p (c i) j -> p c j i", i=4),
                 in_=src.rearrange("p j (c i) -> p c j i", i=4),
             )
 
-        def round_weight(raws, width, name):
+        def round_weight(raws, width, name, copy=nc.scalar.copy):
             grouped = held([P, PASSES, width, PACK], BF16, name + "_grouped")
             for a in range(PASSES):
-                interleave(grouped[:, a], raws[a][:])
+                interleave(grouped[:, a], raws[a], copy)
             return grouped[:].rearrange("p a c j -> p (a c j)")
 
         def quantise(flat, width, name):
@@ -136,9 +146,14 @@ def tile_list_folio_condition_page_kernel(
             nc.vector.quantize_mx(out=codes[:].bitcast(FP8X4), scales=plane[:], in_=flat)
             return codes, plane
 
-        vec_ps = psum.tile([P, S], F32, name="acc")
-        nc.tensor.transpose(vec_ps[:, 0:P], vec_rows[:], ident[:])
-        vecs = held([P, 3 * TILES], F32, "vecs")
+        def turn_vectors(rows, count, name):
+            bank = psum.tile([P, S], F32, name="acc")
+            nc.tensor.transpose(bank[:, 0:P], rows[:], ident[:])
+            cols = held([P, count * TILES], F32, name)
+            nc.scalar.copy(out=cols[:], in_=bank[:, 0 : count * TILES])
+            return cols
+
+        gain_cols = turn_vectors(gain_rows, 1, "gain_cols")
 
         v_w = [held([P, S], U32, "v_w%d" % a) for a in range(PASSES)]
         v_s = held([P, S], U8, "v_s")
@@ -146,18 +161,27 @@ def tile_list_folio_condition_page_kernel(
         wa_q = {}
         wc_q = {}
 
-        def prep_wa(c):
-            width = WA_CHUNKS[c][1]
-            flat = round_weight(wa_raw[c], width, "wa%d" % c)
-            if c == 0:
+        def chunk_of(t):
+            for c, (c0, width) in enumerate(WA_CHUNKS):
+                if c0 <= t * P < c0 + width:
+                    return c, t * P - c0
+
+        def prep_wa(t0, tiles, copy=nc.scalar.copy):
+            c, off = chunk_of(t0)
+            width = tiles * P
+            name = "wa%d" % t0
+            flat = round_weight([raw[:, :, off : off + width] for raw in wa_raw[c]], width, name, copy)
+            if t0 == 0:
                 parts = [quantise(flat[:, a * width * PACK : (a + 1) * width * PACK], width, "wa0_%d" % a) for a in range(PASSES)]
-                wa_q[c] = [(codes[:], plane[:]) for codes, plane in parts]
-            else:
-                codes, plane = quantise(flat, PASSES * width, "wa%d" % c)
-                wa_q[c] = [(codes[:, a * width : (a + 1) * width], plane[:, a * width : (a + 1) * width]) for a in range(PASSES)]
+                wa_q[0] = [(codes[:], plane[:]) for codes, plane in parts]
+                return
+            codes, plane = quantise(flat, PASSES * width, name)
+            for n in range(tiles):
+                cols = [slice(a * width + n * P, a * width + (n + 1) * P) for a in range(PASSES)]
+                wa_q[t0 + n] = [(codes[:, cols[a]], plane[:, cols[a]]) for a in range(PASSES)]
 
         def prep_wc(c):
-            wc_q[c] = quantise(round_weight(wc_raw[c], WC_CHUNK, "wc%d" % c), PASSES * WC_CHUNK, "wc%d" % c)
+            wc_q[c] = quantise(round_weight([raw[:] for raw in wc_raw[c]], WC_CHUNK, "wc%d" % c), PASSES * WC_CHUNK, "wc%d" % c)
 
         def load_wc(c):
             tags = [WC_RAW_TAGS[c] % a for a in range(PASSES)]
@@ -165,32 +189,23 @@ def tile_list_folio_condition_page_kernel(
 
         nc.vector.tensor_copy(v_s[:], tab_s[:].indirect(list1[:]))
         nc.vector.tensor_copy(v_w[1][:], tab_w[1][:].indirect(list1[:]))
-        prep_wa(0)
-        nc.scalar.copy(out=vecs[:], in_=vec_ps[:, 0 : 3 * TILES])
-
-        def chunk_of(t):
-            for c, (c0, width) in enumerate(WA_CHUNKS):
-                if c0 <= t * P < c0 + width:
-                    return c, t * P - c0, width
+        prep_wa(0, 1)
 
         first = {}
-        abs_a = held([P, TILES, S], F32, "abs_a", tag="abs_then_same")
+        abs_a = held([P, TILES, S], F32, "abs_a")
 
         def stage1(t):
-            c, off, width = chunk_of(t)
+            c, off = chunk_of(t)
             acc_b = psum.tile([P, S], F32, name="acc")
             acc_a = psum.tile([P, S], F32, name="acc")
-            for a in range(PASSES):
+            steps = [(a, w) for a in range(PASSES) for w in "ba"] if t == 0 else [(a, w) for w in "ba" for a in range(PASSES)]
+            for a, w in steps:
+                if w == "b":
+                    acc, codes, plane = acc_b, wb_w[c][:, a, off : off + P], wb_s[4 * a : P, t * P : (t + 1) * P]
+                else:
+                    acc, codes, plane = (acc_a, *wa_q[t][a])
                 nc.tensor.matmul_mx(
-                    out=acc_b[:], lhsT=wb_w[c][:, a, off : off + P].bitcast(FP8X4),
-                    lhsT_scale=wb_s[4 * a : P, t * P : (t + 1) * P],
-                    rhs=v_w[a][:].bitcast(FP8X4), rhs_scale=v_s[4 * a : P, :],
-                    start=(a == 0), stop=(a == PASSES - 1),
-                )
-            for a in range(PASSES):
-                codes, plane = wa_q[c][a]
-                nc.tensor.matmul_mx(
-                    out=acc_a[:], lhsT=codes[:, off : off + P].bitcast(FP8X4), lhsT_scale=plane[:, off : off + P],
+                    out=acc[:], lhsT=codes.bitcast(FP8X4), lhsT_scale=plane,
                     rhs=v_w[a][:].bitcast(FP8X4), rhs_scale=v_s[4 * a : P, :],
                     start=(a == 0), stop=(a == PASSES - 1),
                 )
@@ -202,50 +217,83 @@ def tile_list_folio_condition_page_kernel(
         picked = {}
 
         def change_page(t):
-            if t in (1, 2, 3):
-                h = held([P, S], F32, "h%d" % t, tag="wa%d_grouped" % (t + 1))
+            if t == TILES - 1:
+                entry = late.tile([P, S], F32, name="entry_last", align_bytes=64, offset=0)
             else:
-                h = ring.tile([P, S], F32, name="h")
-            nc.vector.scalar_tensor_tensor(
-                out=h[:], in0=first[t][:], scalar=vecs[:, t : t + 1], in1=abs_a[:, t, :], op0=ALU.mult, op1=ALU.subtract
-            )
-            if t >= 1:
-                pick(t - 1)
-            nc.vector.tensor_tensor(pages[t][:].indirect(list2[:]), h[:], wgs_sb[:], ALU.mult)
+                entry = ring.tile([P, S], F32, name="entry")
+            silu_b = first[t]
+            gain_col = gain_cols[:, t : t + 1]
+            if t == 0:
+                h = held([P, S], F32, "h0")
+                nc.vector.scalar_tensor_tensor(
+                    out=h[:], in0=silu_b[:], scalar=gain_col, in1=abs_a[:, t, :], op0=ALU.mult, op1=ALU.subtract
+                )
+                nc.vector.tensor_tensor(entry[:], h[:], wgs_sb[:], ALU.mult)
+            else:
+                nc.gpsimd.tensor_scalar(silu_b[:], silu_b[:], gain_col, 0.0, ALU.mult, ALU.add)
+                nc.gpsimd.tensor_tensor(silu_b[:], silu_b[:], abs_a[:, t, :], ALU.subtract)
+                nc.gpsimd.tensor_tensor(entry[:], silu_b[:], wgs_sb[:], ALU.mult)
+            nc.vector.tensor_copy(pages[t][:].indirect(list2[:]), entry[:])
 
         def pick(t):
-            picked[t] = held([P, NP], F32, "picked%d" % t, tag="silu%d" % (t + 1))
-            nc.vector.tensor_copy(picked[t][:], pages[t][:].indirect(list3[:]))
+            picked[t] = held([P, NP], F32, "picked%d" % t, tag="wa%d_grouped" % (2 * t + 2) if t < 3 else "silu%d" % (t + 1))
+            if t < TILES - 1:
+                nc.vector.tensor_copy(picked[t][:], pages[t][:].indirect(list3[:]))
+            else:
+                for half in range(2):
+                    offsets = list3[:, half * HALF // 16 : (half + 1) * HALF // 16]
+                    nc.vector.tensor_copy(picked[t][:, half * HALF : (half + 1) * HALF], pages[t][:].indirect(offsets))
 
         x_rows = {}
         x_nat = {}
 
         def scale_x(t):
             b, u = divmod(t, QUADS)
+            parts = 1 + b
+            width = NP // parts
             if u == 0:
-                x_nat[b] = held([P, QUADS, NP], BF16, "x_nat%d" % b, tag="wa_raw4_%d" % (1 - b))
-            nc.scalar.activation(out=x_nat[b][:, u, :], in_=picked[t][:], func=ACT.Copy, scale=vecs[:, TILES + t : TILES + t + 1])
-            if u == 0:
-                x_rows[b] = held([P, PACK, NP], BF16, "x_rows%d" % b, tag="wa_raw%d_0" % (2 + b))
-            nc.sync.dma_start(out=x_rows[b][32 * u : 32 * (u + 1)].rearrange("p j n -> p (j n)"), in_=x_nat[b][:, u, :])
+                x_nat[b] = held([P, QUADS, NP], BF16, "x_nat%d" % b, tag=("wa_raw3_1", "wa_raw2_0")[b])
+                x_rows[b] = held([P, parts, PACK * width], BF16, "x_rows%d" % b, tag="wa_raw%d_0" % (2 + b))
+            curl_col = later_cols[:, t : t + 1]
+            last = t == TILES - 1
+            if not last:
+                nc.scalar.activation(out=x_nat[b][:, u, :], in_=picked[t][:], func=ACT.Copy, scale=curl_col)
+            for part in range(parts):
+                cols = slice(part * width, (part + 1) * width)
+                if last:
+                    nc.scalar.activation(out=x_nat[b][:, u, cols], in_=picked[t][:, cols], func=ACT.Copy, scale=curl_col)
+                queue = nc.scalar if last else nc.sync
+                queue.dma_start(out=x_rows[b][32 * u : 32 * (u + 1), part, :], in_=x_nat[b][:, u, cols])
 
         x_q = {}
 
-        def quantise_x(b):
-            grouped = held([P, NP, PACK], BF16, "x_grouped%d" % b, tag="wa_raw%d_1" % (2 + b))
-            interleave(grouped[:], x_rows[b][:])
-            x_q[b] = quantise(grouped[:].rearrange("p n j -> p (n j)"), NP, "x%d" % b)
+        def quantise_x(b, part, tag):
+            width = NP // (1 + b)
+            if b == 0:
+                grouped = late.tile([P, width, PACK], BF16, name="x_grouped0", align_bytes=64, offset=4 * S)
+            else:
+                grouped = held([P, width, PACK], BF16, "x_grouped1_%d" % part, tag=tag)
+            interleave(grouped[:], x_rows[b][:, part, :].rearrange("p (j n) -> p j n", j=PACK))
+            x_q[b, part] = quantise(grouped[:].rearrange("p n j -> p (n j)"), width, "x%d_%d" % (b, part))
 
         stage1(0)
-        prep_wa(1)
+        prep_wa(1, 1, nc.vector.tensor_copy)
         stage1(1)
-        for t in range(TILES):
-            if t in (1, 2, 3):
-                prep_wa(t + 1)
+        change_page(0)
+        prep_wa(2, 1)
+        pick(0)
+        stage1(2)
+        prep_wa(3, 1)
+        for t in range(1, TILES):
             change_page(t)
-            if t >= 1 and t + 1 < TILES:
-                stage1(t + 1)
+            if t in (1, 2):
+                prep_wa(2 * t + 2, 2)
+            if t + 2 < TILES:
+                stage1(t + 2)
+            if t >= 2:
+                pick(t - 1)
         pick(TILES - 1)
+        later_cols = turn_vectors(later_rows, 2, "later_cols")
         for c in range(H // WC_CHUNK):
             load_wc(c)
         wd_w = held([P, PASSES, 2 * H], U8, "wd_w")
@@ -255,11 +303,15 @@ def tile_list_folio_condition_page_kernel(
                 out=wd_s[32 * q : 32 * q + 4, :, :].bitcast(I32),
                 in_=wd_scales[:, 4 * q : 4 * q + 4, :].rearrange("a r c -> r a c").bitcast(I32),
             )
-        for c in range(H // WC_CHUNK):
-            prep_wc(c)
-        for t in range(TILES):
+        prep_wc(0)
+        prep_wc(1)
+        for t in range(QUADS):
             scale_x(t)
-        quantise_x(0)
+        quantise_x(0, 0, None)
+        prep_wc(2)
+        prep_wc(3)
+        for t in range(QUADS, TILES):
+            scale_x(t)
 
         same = {}
 
@@ -267,32 +319,31 @@ def tile_list_folio_condition_page_kernel(
             same[t] = tile
             nc.vector.tensor_copy(tile, pages[t][:].indirect(list4[:]))
 
-        same_a = held([P, 2, NP], F32, "same_a", tag="abs_then_same")
-        same_b = held([P, 2, NP], F32, "same_b", tag="wa_raw2_1")
-        for t in range(2):
+        same_a = late.tile([P, FREE_PICKS, NP], F32, name="same_a", align_bytes=64, offset=0)
+        for t in range(FREE_PICKS):
             pick_same(t, same_a[:, t, :])
-        for t in range(2):
-            pick_same(2 + t, same_b[:, t, :])
         second = {}
 
-        def stage2(t, b):
+        def stage2(t, b, part):
             if b == 0:
                 second[t] = (psum.tile([P, NP], F32, name="acc"), psum.tile([P, NP], F32, name="acc"))
             y1, y2 = second[t]
             c, off = divmod(t * P, WC_CHUNK)
             codes, plane = wc_q[c]
-            x_codes, x_plane = x_q[b]
+            x_codes, x_plane = x_q[b, part]
+            width = NP // (1 + b)
+            tokens = slice(part * width, (part + 1) * width)
             cols = slice(b * WC_CHUNK + off, b * WC_CHUNK + off + P)
             nc.tensor.matmul_mx(
-                out=y2[:], lhsT=wd_w[:, b, 2 * t * P : 2 * (t + 1) * P].bitcast(FP4X4),
+                out=y2[:, tokens], lhsT=wd_w[:, b, 2 * t * P : 2 * (t + 1) * P].bitcast(FP4X4),
                 lhsT_scale=wd_s[:, b, t * P : (t + 1) * P],
                 rhs=x_codes[:].bitcast(FP8X4), rhs_scale=x_plane[:],
-                start=(b == 0), stop=(b == PASSES - 1),
+                start=(b == 0), stop=(b == 1 and part == 1),
             )
             nc.tensor.matmul_mx(
-                out=y1[:], lhsT=codes[:, cols].bitcast(FP8X4), lhsT_scale=plane[:, cols],
+                out=y1[:, tokens], lhsT=codes[:, cols].bitcast(FP8X4), lhsT_scale=plane[:, cols],
                 rhs=x_codes[:].bitcast(FP8X4), rhs_scale=x_plane[:],
-                start=(b == 0), stop=(b == PASSES - 1),
+                start=(b == 0), stop=(b == 1 and part == 1),
             )
 
         def finish(t):
@@ -301,7 +352,7 @@ def tile_list_folio_condition_page_kernel(
             nc.scalar.activation(out=abs_y2[:], in_=y2[:], func=ACT.Abs)
             top = ring.tile([P, NP], F32, name="top", bufs=4)
             nc.vector.scalar_tensor_tensor(
-                out=top[:], in0=same[t], scalar=vecs[:, 2 * TILES + t : 2 * TILES + t + 1], in1=y1[:],
+                out=top[:], in0=same[t], scalar=later_cols[:, TILES + t : TILES + t + 1], in1=y1[:],
                 op0=ALU.mult, op1=ALU.max,
             )
             res = held([P, NP], F32, "res%d" % t, tag="wc%d_grouped" % (t % 4))
@@ -311,15 +362,19 @@ def tile_list_folio_condition_page_kernel(
 
         early = TILES // 2
         for t in range(early):
-            stage2(t, 0)
-        quantise_x(1)
-        pick_same(4, held([P, NP], F32, "same_c", tag="wa_raw3_1")[:])
-        for t in range(early):
-            stage2(t, 1)
+            stage2(t, 0, 0)
+        quantise_x(1, 0, "wa_raw3_1")
+        pick_same(FREE_PICKS, held([P, NP], F32, "same_b", tag="wa_raw3_1")[:])
+        quantise_x(1, 1, "wa_raw2_1")
+        pick_same(FREE_PICKS + 1, held([P, NP], F32, "same_c", tag="wa_raw2_1")[:])
+        for part in range(2):
+            for t in range(early):
+                stage2(t, 1, part)
         for t in range(TILES):
             if t >= early:
-                stage2(t, 0)
-                stage2(t, 1)
+                stage2(t, 0, 0)
+                stage2(t, 1, 0)
+                stage2(t, 1, 1)
             finish(t)
-            if t + 5 < TILES:
-                pick_same(t + 5, same[t])
+            if t + FREE_PICKS + 2 < TILES:
+                pick_same(t + FREE_PICKS + 2, same[t])

from contextlib import ExitStack

import concourse.mybir as mybir
from concourse.masks import make_identity

K, H, T, S, T2, NP = 1024, 1024, 2048, 512, 1024, 512
FLOPS = 4 * 2 * K * H * S

F32 = mybir.dt.float32
BF16 = mybir.dt.bfloat16
I32 = mybir.dt.int32
U32 = mybir.dt.uint32
U16 = mybir.dt.uint16
U8 = mybir.dt.uint8
FP8X4 = mybir.dt.float8_e4m3fn_x4
FP4X4 = mybir.dt.float4_e2m1fn_x4
ALU = mybir.AluOpType
ACT = mybir.ActivationFunctionType

P = 128
PACK = 4
KP = P * PACK
PASSES = K // KP
TILES = H // P
QUADS = 4
WA_CHUNKS = [(0, 128), (128, 128), (256, 256), (512, 256), (768, 256)]
WC_CHUNK = 256
GPSIMD_SUBS = 6
HALF = NP // 2
FREE_PICKS = 3
WC_RAW_TAGS = ["wa_raw2_%d", "wa_raw3_%d", "wc_raw2_%d", "wa_raw4_%d"]


def tile_list_folio_condition_page_kernel(
    tc, tab_words, tab_scales, offs, wa, wb_words, wb_scales, gain, page0, wgs,
    offs2, offs3, curl, wc, wd_words, wd_scales, offs4, quire, out,
):
    nc = tc.nc
    with ExitStack() as ctx:
        keep = ctx.enter_context(tc.tile_pool(name="keep", bufs=1))
        ring = ctx.enter_context(tc.tile_pool(name="ring", bufs=2))
        late = ctx.enter_context(tc.tile_pool(name="late", bufs=1))
        psum = ctx.enter_context(tc.psum_pool(name="psum", bufs=8))

        def held(shape, dtype, name, tag=None):
            return keep.tile(shape, dtype, name=name, tag=tag or name, align_bytes=64)

        def load_list(src, name):
            lst = held([P, S // 16], U16, name)
            nc.sync.dma_start(lst[:], src)
            return lst

        def load_raw(w, a, c0, width, name, tag=None):
            raw = held([P, PACK, width], F32, name, tag)
            rows = w[a * KP : (a + 1) * KP, c0 : c0 + width]
            nc.sync.dma_start(out=raw[:], in_=rows.rearrange("(p j) c -> p j c", j=PACK))
            return raw

        def load_tab_words(a):
            words = held([P, T], U32, "tab_w%d" % a)
            nc.sync.dma_start(out=words[:].bitcast(I32), in_=tab_words[a].rearrange("p t i -> p (t i)").bitcast(I32))
            return words

        def load_wb_words(c):
            c0, width = WA_CHUNKS[c]
            words = held([P, PASSES, width], U32, "wb_w%d" % c)
            src = wb_words[:, :, c0 : c0 + width, :].rearrange("a p c i -> p a (c i)")
            nc.sync.dma_start(out=words[:].bitcast(I32), in_=src.bitcast(I32))
            return words

        def load_page(t):
            page = held([P, T2], F32, "page%d" % t)
            nc.sync.dma_start(out=page[:], in_=page0[t * P : (t + 1) * P, :])
            return page

        def load_packed_scales(engine, plane, scales):
            for q in range(QUADS):
                engine.dma_start(
                    out=plane[32 * q : 32 * q + 4 * PASSES, :].bitcast(I32),
                    in_=scales[:, 4 * q : 4 * q + 4, :].bitcast(I32),
                )

        tab_s = held([P, T], U8, "tab_s")
        nc.vector.memset(tab_s[:].bitcast(I32), 0)
        def load_vectors(vectors, name):
            rows = held([P, P], F32, name)
            nc.gpsimd.memset(rows[:], 0.0)
            for n, vec in enumerate(vectors):
                nc.gpsimd.dma_start(out=rows[TILES * n : TILES * (n + 1), :], in_=vec.rearrange("(t p) -> t p", p=P))
            return rows

        gain_rows = load_vectors([gain], "gain_rows")
        ident = held([P, P], F32, "ident")
        make_identity(nc, ident[:])
        later_rows = load_vectors([curl, quire], "later_rows")
        wb_s = held([P, H], U8, "wb_s")
        nc.vector.memset(wb_s[:].bitcast(I32), 0)
        wd_s = held([P, PASSES, H], U8, "wd_s")
        nc.vector.memset(wd_s[:].rearrange("p a c -> p (a c)").bitcast(I32), 0)

        list1 = load_list(offs, "list1")
        tab_w = [load_tab_words(0)]
        load_packed_scales(nc.sync, tab_s, tab_scales)
        wa_raw = [[load_raw(wa, 0, 0, WA_CHUNKS[0][1], "wa_raw0_0")]]
        wb_w = [load_wb_words(0)]
        tab_w.append(load_tab_words(1))
        load_packed_scales(nc.sync, wb_s, wb_scales)
        wa_raw[0].append(load_raw(wa, 1, 0, WA_CHUNKS[0][1], "wa_raw0_1"))

        def load_wa(c):
            c0, width = WA_CHUNKS[c]
            wa_raw.append([load_raw(wa, a, c0, width, "wa_raw%d_%d" % (c, a)) for a in range(PASSES)])
            wb_w.append(load_wb_words(c))

        load_wa(1)
        list2 = load_list(offs2, "list2")
        wgs_sb = held([P, S], F32, "wgs_sb")
        nc.sync.dma_start(out=wgs_sb[:], in_=wgs)
        pages = [load_page(0)]
        list3 = load_list(offs3, "list3")
        wc_raw = []
        load_wa(2)
        pages.append(load_page(1))
        load_wa(3)
        pages.append(load_page(2))
        load_wa(4)
        for t in range(3, TILES):
            pages.append(load_page(t))
        list4 = load_list(offs4, "list4")

        def interleave(dst, src, copy=nc.scalar.copy):
            copy(
                out=dst.rearrange("p (c i) j -> p c j i", i=4),
                in_=src.rearrange("p j (c i) -> p c j i", i=4),
            )

        def round_weight(raws, width, name, copy=nc.scalar.copy):
            grouped = held([P, PASSES, width, PACK], BF16, name + "_grouped")
            for a in range(PASSES):
                interleave(grouped[:, a], raws[a], copy)
            return grouped[:].rearrange("p a c j -> p (a c j)")

        def quantise(flat, width, name):
            codes = held([P, width], U32, name + "_codes")
            plane = held([P, width], U8, name + "_plane")
            nc.vector.quantize_mx(out=codes[:].bitcast(FP8X4), scales=plane[:], in_=flat)
            return codes, plane

        def turn_vectors(rows, count, name):
            bank = psum.tile([P, S], F32, name="acc")
            nc.tensor.transpose(bank[:, 0:P], rows[:], ident[:])
            cols = held([P, count * TILES], F32, name)
            nc.scalar.copy(out=cols[:], in_=bank[:, 0 : count * TILES])
            return cols

        gain_cols = turn_vectors(gain_rows, 1, "gain_cols")

        v_w = [held([P, S], U32, "v_w%d" % a) for a in range(PASSES)]
        v_s = held([P, S], U8, "v_s")
        nc.vector.tensor_copy(v_w[0][:], tab_w[0][:].indirect(list1[:]))
        wa_q = {}
        wc_q = {}

        def chunk_of(t):
            for c, (c0, width) in enumerate(WA_CHUNKS):
                if c0 <= t * P < c0 + width:
                    return c, t * P - c0

        def prep_wa(t0, tiles, copy=nc.scalar.copy):
            c, off = chunk_of(t0)
            width = tiles * P
            name = "wa%d" % t0
            flat = round_weight([raw[:, :, off : off + width] for raw in wa_raw[c]], width, name, copy)
            if t0 == 0:
                parts = [quantise(flat[:, a * width * PACK : (a + 1) * width * PACK], width, "wa0_%d" % a) for a in range(PASSES)]
                wa_q[0] = [(codes[:], plane[:]) for codes, plane in parts]
                return
            codes, plane = quantise(flat, PASSES * width, name)
            for n in range(tiles):
                cols = [slice(a * width + n * P, a * width + (n + 1) * P) for a in range(PASSES)]
                wa_q[t0 + n] = [(codes[:, cols[a]], plane[:, cols[a]]) for a in range(PASSES)]

        def prep_wc(c):
            wc_q[c] = quantise(round_weight([raw[:] for raw in wc_raw[c]], WC_CHUNK, "wc%d" % c), PASSES * WC_CHUNK, "wc%d" % c)

        def load_wc(c):
            tags = [WC_RAW_TAGS[c] % a for a in range(PASSES)]
            wc_raw.append([load_raw(wc, a, c * WC_CHUNK, WC_CHUNK, "wc_raw%d_%d" % (c, a), tags[a]) for a in range(PASSES)])

        nc.vector.tensor_copy(v_s[:], tab_s[:].indirect(list1[:]))
        nc.vector.tensor_copy(v_w[1][:], tab_w[1][:].indirect(list1[:]))
        prep_wa(0, 1)

        first = {}
        abs_a = held([P, TILES, S], F32, "abs_a")

        def stage1(t):
            c, off = chunk_of(t)
            acc_b = psum.tile([P, S], F32, name="acc")
            acc_a = psum.tile([P, S], F32, name="acc")
            steps = [(a, w) for a in range(PASSES) for w in "ba"] if t == 0 else [(a, w) for w in "ba" for a in range(PASSES)]
            for a, w in steps:
                if w == "b":
                    acc, codes, plane = acc_b, wb_w[c][:, a, off : off + P], wb_s[4 * a : P, t * P : (t + 1) * P]
                else:
                    acc, codes, plane = (acc_a, *wa_q[t][a])
                nc.tensor.matmul_mx(
                    out=acc[:], lhsT=codes.bitcast(FP8X4), lhsT_scale=plane,
                    rhs=v_w[a][:].bitcast(FP8X4), rhs_scale=v_s[4 * a : P, :],
                    start=(a == 0), stop=(a == PASSES - 1),
                )
            silu_b = held([P, S], F32, "silu%d" % t)
            nc.scalar.activation(out=silu_b[:], in_=acc_b[:], func=ACT.Silu)
            nc.scalar.activation(out=abs_a[:, t, :], in_=acc_a[:], func=ACT.Abs)
            first[t] = silu_b

        picked = {}

        def change_page(t):
            if t == TILES - 1:
                entry = late.tile([P, S], F32, name="entry_last", align_bytes=64, offset=0)
            else:
                entry = ring.tile([P, S], F32, name="entry")
            silu_b = first[t]
            gain_col = gain_cols[:, t : t + 1]
            if t == 0:
                h = held([P, S], F32, "h0")
                nc.vector.scalar_tensor_tensor(
                    out=h[:], in0=silu_b[:], scalar=gain_col, in1=abs_a[:, t, :], op0=ALU.mult, op1=ALU.subtract
                )
                nc.vector.tensor_tensor(entry[:], h[:], wgs_sb[:], ALU.mult)
            else:
                nc.gpsimd.tensor_scalar(silu_b[:], silu_b[:], gain_col, 0.0, ALU.mult, ALU.add)
                nc.gpsimd.tensor_tensor(silu_b[:], silu_b[:], abs_a[:, t, :], ALU.subtract)
                nc.gpsimd.tensor_tensor(entry[:], silu_b[:], wgs_sb[:], ALU.mult)
            nc.vector.tensor_copy(pages[t][:].indirect(list2[:]), entry[:])

        def pick(t):
            picked[t] = held([P, NP], F32, "picked%d" % t, tag="wa%d_grouped" % (2 * t + 2) if t < 3 else "silu%d" % (t + 1))
            if t < TILES - 1:
                nc.vector.tensor_copy(picked[t][:], pages[t][:].indirect(list3[:]))
            else:
                for half in range(2):
                    offsets = list3[:, half * HALF // 16 : (half + 1) * HALF // 16]
                    nc.vector.tensor_copy(picked[t][:, half * HALF : (half + 1) * HALF], pages[t][:].indirect(offsets))

        x_rows = {}
        x_nat = {}

        def scale_x(t):
            b, u = divmod(t, QUADS)
            parts = 1 + b
            width = NP // parts
            if u == 0:
                x_nat[b] = held([P, QUADS, NP], BF16, "x_nat%d" % b, tag=("wa_raw3_1", "wa_raw2_0")[b])
                x_rows[b] = held([P, parts, PACK * width], BF16, "x_rows%d" % b, tag="wa_raw%d_0" % (2 + b))
            curl_col = later_cols[:, t : t + 1]
            last = t == TILES - 1
            if not last:
                nc.scalar.activation(out=x_nat[b][:, u, :], in_=picked[t][:], func=ACT.Copy, scale=curl_col)
            for part in range(parts):
                cols = slice(part * width, (part + 1) * width)
                if last:
                    nc.scalar.activation(out=x_nat[b][:, u, cols], in_=picked[t][:, cols], func=ACT.Copy, scale=curl_col)
                queue = nc.scalar if last else nc.sync
                queue.dma_start(out=x_rows[b][32 * u : 32 * (u + 1), part, :], in_=x_nat[b][:, u, cols])

        x_q = {}

        def quantise_x(b, part, tag):
            width = NP // (1 + b)
            if b == 0:
                grouped = late.tile([P, width, PACK], BF16, name="x_grouped0", align_bytes=64, offset=4 * S)
            else:
                grouped = held([P, width, PACK], BF16, "x_grouped1_%d" % part, tag=tag)
            interleave(grouped[:], x_rows[b][:, part, :].rearrange("p (j n) -> p j n", j=PACK))
            x_q[b, part] = quantise(grouped[:].rearrange("p n j -> p (n j)"), width, "x%d_%d" % (b, part))

        stage1(0)
        prep_wa(1, 1, nc.vector.tensor_copy)
        stage1(1)
        change_page(0)
        prep_wa(2, 1)
        pick(0)
        stage1(2)
        prep_wa(3, 1)
        for t in range(1, TILES):
            change_page(t)
            if t in (1, 2):
                prep_wa(2 * t + 2, 2)
            if t + 2 < TILES:
                stage1(t + 2)
            if t >= 2:
                pick(t - 1)
        pick(TILES - 1)
        later_cols = turn_vectors(later_rows, 2, "later_cols")
        for c in range(H // WC_CHUNK):
            load_wc(c)
        wd_w = held([P, PASSES, 2 * H], U8, "wd_w")
        nc.sync.dma_start(out=wd_w[:].bitcast(I32), in_=wd_words.rearrange("a p c -> p a c").bitcast(I32))
        for q in range(QUADS):
            nc.sync.dma_start(
                out=wd_s[32 * q : 32 * q + 4, :, :].bitcast(I32),
                in_=wd_scales[:, 4 * q : 4 * q + 4, :].rearrange("a r c -> r a c").bitcast(I32),
            )
        prep_wc(0)
        prep_wc(1)
        for t in range(QUADS):
            scale_x(t)
        quantise_x(0, 0, None)
        prep_wc(2)
        prep_wc(3)
        for t in range(QUADS, TILES):
            scale_x(t)

        same = {}

        def pick_same(t, tile):
            same[t] = tile
            nc.vector.tensor_copy(tile, pages[t][:].indirect(list4[:]))

        same_a = late.tile([P, FREE_PICKS, NP], F32, name="same_a", align_bytes=64, offset=0)
        for t in range(FREE_PICKS):
            pick_same(t, same_a[:, t, :])
        second = {}

        def stage2(t, b, part):
            if b == 0:
                second[t] = (psum.tile([P, NP], F32, name="acc"), psum.tile([P, NP], F32, name="acc"))
            y1, y2 = second[t]
            c, off = divmod(t * P, WC_CHUNK)
            codes, plane = wc_q[c]
            x_codes, x_plane = x_q[b, part]
            width = NP // (1 + b)
            tokens = slice(part * width, (part + 1) * width)
            cols = slice(b * WC_CHUNK + off, b * WC_CHUNK + off + P)
            nc.tensor.matmul_mx(
                out=y2[:, tokens], lhsT=wd_w[:, b, 2 * t * P : 2 * (t + 1) * P].bitcast(FP4X4),
                lhsT_scale=wd_s[:, b, t * P : (t + 1) * P],
                rhs=x_codes[:].bitcast(FP8X4), rhs_scale=x_plane[:],
                start=(b == 0), stop=(b == 1 and part == 1),
            )
            nc.tensor.matmul_mx(
                out=y1[:, tokens], lhsT=codes[:, cols].bitcast(FP8X4), lhsT_scale=plane[:, cols],
                rhs=x_codes[:].bitcast(FP8X4), rhs_scale=x_plane[:],
                start=(b == 0), stop=(b == 1 and part == 1),
            )

        def finish(t):
            y1, y2 = second[t]
            abs_y2 = held([P, NP], F32, "abs_y2_%d" % t, tag="silu%d" % t)
            nc.scalar.activation(out=abs_y2[:], in_=y2[:], func=ACT.Abs)
            top = ring.tile([P, NP], F32, name="top", bufs=4)
            nc.vector.scalar_tensor_tensor(
                out=top[:], in0=same[t], scalar=later_cols[:, TILES + t : TILES + t + 1], in1=y1[:],
                op0=ALU.mult, op1=ALU.max,
            )
            res = held([P, NP], F32, "res%d" % t, tag="wc%d_grouped" % (t % 4))
            engine = nc.gpsimd if t < GPSIMD_SUBS else nc.vector
            engine.tensor_tensor(res[:], top[:], abs_y2[:], ALU.subtract)
            nc.sync.dma_start(out=out[t * P : (t + 1) * P, :], in_=res[:])

        early = TILES // 2
        for t in range(early):
            stage2(t, 0, 0)
        quantise_x(1, 0, "wa_raw3_1")
        pick_same(FREE_PICKS, held([P, NP], F32, "same_b", tag="wa_raw3_1")[:])
        quantise_x(1, 1, "wa_raw2_1")
        pick_same(FREE_PICKS + 1, held([P, NP], F32, "same_c", tag="wa_raw2_1")[:])
        for part in range(2):
            for t in range(early):
                stage2(t, 1, part)
        for t in range(TILES):
            if t >= early:
                stage2(t, 0, 0)
                stage2(t, 1, 0)
                stage2(t, 1, 1)
            finish(t)
            if t + FREE_PICKS + 2 < TILES:
                pick_same(t + FREE_PICKS + 2, same[t])
